import numpy as np
import ml_dtypes


def mxq(x, axis, fmt="e4m3"):
    dtype, down = {"e4m3": (ml_dtypes.float8_e4m3fn, 7), "e5m2": (ml_dtypes.float8_e5m2, 14)}[fmt]
    v = np.moveaxis(np.asarray(x, np.float32).astype(ml_dtypes.bfloat16).astype(np.float64), axis, -1)
    blocks = v.reshape(v.shape[:-1] + (-1, 32))
    amax = np.abs(blocks).max(-1, keepdims=True)
    byte = np.maximum(np.where(amax > 0, np.frexp(amax)[1] - 1 + 127, 0) - down, 1)
    scale = np.exp2(byte - 127.0)
    codes = (blocks / scale).astype(np.float32).astype(dtype).astype(np.float64)
    return np.moveaxis((codes * scale).reshape(v.shape), -1, axis)


WIDE = False


def mx_kscale(k):
    if not WIDE:
        return np.ones(k)
    levels = np.array([10, -10, 5, -5, 0])
    if k % 512:
        return np.exp2(np.random.permutation(np.resize(levels, k // 32))).repeat(32)
    a = np.empty((k // 512, 16))
    for p in range(k // 512):
        a[p, :8] = np.random.permutation(np.resize(levels, 8))
        for g in range(8):
            far = levels[np.abs(levels - a[p, g]) >= 10]
            a[p, g + 8] = far[np.random.randint(len(far))]
    return np.exp2(a.ravel()).repeat(32)


def f64(x):
    return np.asarray(x).astype(np.float64)


def striped(idx):
    return np.tile(idx.reshape(-1, 16).T, (8, 1)).astype(np.uint16)


def unstriped(offs):
    return offs[:16].T.reshape(-1).astype(np.int64)


def striped8(idx):
    return np.concatenate([x.reshape(-1, 16).T for x in idx]).astype(np.uint16)


def runs(offs, k):
    lists = np.stack([offs[16 * r : 16 * r + 16].T.reshape(-1) for r in range(8)]).astype(np.int64)
    return lists[np.arange(k) % 512 // 64]


def pack_weight(w):
    k, n = w.shape
    w = f64(np.asarray(w, np.float32).astype(ml_dtypes.bfloat16)).reshape(k // 32, 32, n)
    amax = np.abs(w).max(1)
    byte = np.clip(np.where(amax > 0, np.frexp(amax)[1] - 1 + 127 - 7, 1), 1, 254)
    scaled = (w * np.exp2(127.0 - byte)[:, None, :]).reshape(k, n).astype(np.float32)
    words = np.ascontiguousarray(scaled.reshape(k // 512, 128, 4, n).transpose(0, 1, 3, 2)).astype(ml_dtypes.float8_e4m3fn).view(np.uint8)
    return words, np.ascontiguousarray(byte.astype(np.uint8).reshape(k // 512, 16, n))


def unpack_weight(words, scales):
    g, p, n, _ = words.shape
    vals = np.ascontiguousarray(words).view(ml_dtypes.float8_e4m3fn).astype(np.float64) * np.repeat(np.exp2(scales.astype(np.float64) - 127.0), 8, axis=1)[..., None]
    return vals.transpose(0, 1, 3, 2).reshape(g * 512, n)


E2M1 = np.array([0.0, 0.5, 1.0, 1.5, 2.0, 3.0, 4.0, 6.0, -0.0, -0.5, -1.0, -1.5, -2.0, -3.0, -4.0, -6.0])


def pack_fp4(w):
    k, n = w.shape
    w = f64(np.asarray(w, np.float32).astype(ml_dtypes.bfloat16)).reshape(k // 32, 32, n)
    amax = np.abs(w).max(1)
    mant, ex = np.frexp(amax / 6.0)
    byte = np.clip(np.where(amax > 0, np.where(mant > 0.5, ex, ex - 1) + 127, 1), 1, 254)
    scaled = (w * np.exp2(127.0 - byte)[:, None, :]).reshape(k, n).astype(np.float32)
    c = np.ascontiguousarray(scaled.reshape(k // 512, 128, 4, n).transpose(0, 1, 3, 2)).astype(ml_dtypes.float4_e2m1fn).view(np.uint8) & 0xF
    words = (c[..., 0::2] | (c[..., 1::2] << 4)).reshape(k // 512, 128, 2 * n)
    return np.ascontiguousarray(words), np.ascontiguousarray(byte.astype(np.uint8).reshape(k // 512, 16, n))


def unpack_fp4(words, scales):
    g, _, n = scales.shape
    words = np.ascontiguousarray(words).reshape(g, 128, n, 2)
    nib = np.empty((g, 128, n, 4), np.uint8)
    nib[..., 0::2] = words & 0xF
    nib[..., 1::2] = words >> 4
    vals = E2M1[nib] * np.repeat(np.exp2(scales.astype(np.float64) - 127.0), 8, axis=1)[..., None]
    return vals.transpose(0, 1, 3, 2).reshape(g * 512, n)


def sigmoid(v):
    return 1.0 / (1.0 + np.exp(-np.maximum(v, -700.0)))


K, T, S, H, W, G = 512, 2048, 256, 512, 128, 2048


def setup_inputs():
    n = np.random.standard_normal
    s = mx_kscale(K)[:, None]
    packed_xT = pack_weight(n((K, T)) * s)
    packed_w1 = pack_fp4(n((K, H)) / np.sqrt(K) / s)
    packed_dT = pack_weight(n((K, G)) / s)
    perm = np.random.permutation(S)
    return {
        "x_words": packed_xT[0],
        "x_scales": packed_xT[1],
        "w1_words": packed_w1[0],
        "w1_scales": packed_w1[1],
        "gs": (np.random.uniform(0.5, 1.5, (K, 1)) * s).astype(np.float32),
        "d_words": packed_dT[0],
        "d_scales": packed_dT[1],
        "sl": np.random.uniform(1.0, 2.0, (H, 1)).astype(np.float32),
        "th": (0.5 * n((H, 1))).astype(np.float32),
        "offs": striped8(np.random.randint(0, T, (8, S))),
        "n1": striped(perm[:W]),
        "n2": striped(perm[W:]),
        "n3": striped(np.random.permutation(S)),
        "k1": striped8(np.random.randint(0, G, (8, H))),
        "n4": striped8(np.stack([np.random.permutation(S) for _ in range(8)])),
        "n5": striped8(np.stack([np.random.permutation(S) for _ in range(8)])),
    }


def reference(x_words, x_scales, w1_words, w1_scales, gs, d_words, d_scales, sl, th, offs, n1, n2, n3, k1, n4, n5):
    d_k1 = unpack_weight(d_words, d_scales)[np.arange(K)[:, None], runs(k1, K)]
    xq = unpack_weight(x_words, x_scales)[np.arange(K)[:, None], runs(offs, K)]
    y = unpack_fp4(w1_words, w1_scales).T @ xq
    pa = y[:, unstriped(n1)]
    pb = y[:, unstriped(n2)]
    rb = pa - pb
    ds = np.zeros((H, S))
    ds[:, unstriped(n1)] = pb
    dt = ds.copy()
    dt[:, unstriped(n2)] = rb
    z = f64(gs) * (np.maximum(dt, 0.5 * dt[:, unstriped(n3)]))
    h = 0.0625 * ((d_k1.T @ mxq(z, 0, "e4m3")))
    st = h - (h[np.arange(H)[:, None], runs(n4, H)])
    sg = sigmoid(f64(sl) * (st[np.arange(H)[:, None], runs(n5, H)] - f64(th)))
    return h * sg

@@ -1,0 +1,240 @@
+from contextlib import ExitStack
+
+import concourse.mybir as mybir
+
+K, T, S, H, W = 512, 2048, 256, 512, 128
+FLOPS = 2 * K * H * S * 2
+
+F32 = mybir.dt.float32
+BF16 = mybir.dt.bfloat16
+I32 = mybir.dt.int32
+U32 = mybir.dt.uint32
+U16 = mybir.dt.uint16
+U8 = mybir.dt.uint8
+FP8X4 = mybir.dt.float8_e4m3fn_x4
+FP4X4 = mybir.dt.float4_e2m1fn_x4
+ALU = mybir.AluOpType
+ACT = mybir.ActivationFunctionType
+
+P = 128
+PACK = 4
+HALF = S // 2
+SPARE = 16
+
+
+def tile_picked_hdenseswapdehq_none_p_kernel(
+    tc, x_words, x_scales, w1_words, w1_scales, gs, d_words, d_scales, sl, th,
+    offs, n1, n2, n3, k1, n4, n5, out,
+):
+    nc = tc.nc
+    with ExitStack() as ctx:
+        lists = ctx.enter_context(tc.tile_pool(name="lists", bufs=1))
+        keep = ctx.enter_context(tc.tile_pool(name="keep", bufs=1))
+        psum = ctx.enter_context(tc.psum_pool(name="psum", bufs=1))
+
+        def load_list(src, name):
+            tile = lists.tile(list(src.shape), U16, name=name)
+            nc.sync.dma_start(tile[:], src)
+            return tile
+
+        def load_words(src, queue, name):
+            tile = keep.tile([P, T], U32, name=name, tag="table_words", align_bytes=64)
+            queue.dma_start(tile[:].bitcast(I32), src[0].rearrange("p c r -> p (c r)").bitcast(I32))
+            return tile
+
+        def load_scale_rows(tile, src, queue):
+            queue.dma_start(tile[0:P:8, :].bitcast(I32), src[0].bitcast(I32))
+
+        def place_rows(plane, picked, queue):
+            for s in range(1, 4):
+                queue.dma_start(plane[s:P:32, :].bitcast(I32), picked[8 * s:P:32, :].bitcast(I32))
+            for q in range(4):
+                nc.vector.tensor_copy(plane[32 * q:32 * q + 1, :].bitcast(I32), picked[32 * q:32 * q + 1, :].bitcast(I32))
+
+        def load_column(src, name, tag):
+            tile = keep.tile([P, PACK], F32, name=name, tag=tag, align_bytes=64)
+            nc.gpsimd.dma_start(tile[:], src.rearrange("(p t) o -> p (t o)", t=PACK))
+            return tile
+
+        w1_scale_raw = keep.tile([P, H], U8, name="w1_scale_raw", tag="w1_scale_raw", align_bytes=64)
+        nc.vector.memset(w1_scale_raw[:].bitcast(I32), 0)
+        x_scale_tab = keep.tile([P, T], U8, name="x_scale_tab", tag="x_scale_tab", align_bytes=64)
+        nc.vector.memset(x_scale_tab[:].bitcast(I32), 0)
+
+        offs_t = load_list(offs, "offs_t")
+        x_word_tab = load_words(x_words, nc.scalar, "x_word_tab")
+        load_scale_rows(x_scale_tab, x_scales, nc.sync)
+        w1_scale_rows = w1_scales[0].bitcast(I32)
+        for q in range(4):
+            queue = nc.sync if q < 3 else nc.gpsimd
+            queue.dma_start(w1_scale_raw[32 * q:32 * q + 4, :].bitcast(I32), w1_scale_rows[4 * q:4 * q + 4, :])
+        w1_word_raw = keep.tile([P, 2 * H], U8, name="w1_word_raw", tag="w1_word_raw", align_bytes=64)
+        nc.sync.dma_start(w1_word_raw[:].bitcast(I32), w1_words[0].bitcast(I32))
+        n2_t = load_list(n2, "n2_t")
+        n1_t = load_list(n1, "n1_t")
+        n3_t = load_list(n3, "n3_t")
+        k1_t = load_list(k1, "k1_t")
+        n4_t = load_list(n4, "n4_t")
+        n5_t = load_list(n5, "n5_t")
+
+        xq_scale = keep.tile([P, S], U8, name="xq_scale", align_bytes=64)
+        nc.vector.memset(xq_scale[:].bitcast(I32), 0)
+        dk_scale = keep.tile([P, H], U8, name="dk_scale", align_bytes=64)
+        nc.vector.memset(dk_scale[:].bitcast(I32), 0)
+        dt = []
+        for t in range(PACK):
+            tile = keep.tile([P, S + SPARE], F32, name="dt%d" % t)
+            nc.vector.memset(tile[:, S:], 0.0)
+            dt.append(tile)
+
+        d_scale_tab = keep.tile([P, T], U8, name="d_scale_tab", align_bytes=64)
+        nc.vector.memset(d_scale_tab[:].bitcast(I32), 0)
+        load_scale_rows(d_scale_tab, d_scales, nc.gpsimd)
+
+        xq_scale_picked = keep.tile([P, S], U8, name="xq_scale_picked", align_bytes=64)
+        nc.vector.tensor_copy(xq_scale_picked[:], x_scale_tab[:].indirect(offs_t[:]))
+        place_rows(xq_scale, xq_scale_picked, nc.scalar)
+
+        w1_scale = keep.tile([P, PACK, P], U8, name="w1_scale", tag="w1_scale", align_bytes=64)
+        nc.vector.tensor_copy(w1_scale[:], w1_scale_raw[:].rearrange("p (m t) -> p t m", t=PACK))
+        w1_word = []
+        for t in range(PACK):
+            tile = keep.tile([P, 2 * P], U8, name="w1_word%d" % t, align_bytes=64)
+            nc.scalar.copy(tile[:].bitcast(U16), w1_word_raw[:].bitcast(U16)[:, t:H:PACK])
+            w1_word.append(tile)
+
+        xq_word = keep.tile([P, S], U32, name="xq_word", align_bytes=64)
+        nc.vector.tensor_copy(xq_word[:], x_word_tab[:].indirect(offs_t[:]))
+        d_word_tab = load_words(d_words, nc.sync, "d_word_tab")
+        gs_t = load_column(gs, "gs_t", "x_scale_tab")
+        sl_t = load_column(sl, "sl_t", "w1_scale_raw")
+        th_t = load_column(th, "th_t", "w1_word_raw")
+
+        y = []
+        for t in range(PACK):
+            bank = psum.tile([P, S], F32, name="y_bank%d" % t, tag="bank%d" % t)
+            nc.tensor.matmul_mx(
+                out=bank[:], lhsT=w1_word[t][:].bitcast(FP4X4), lhsT_scale=w1_scale[:, t, :],
+                rhs=xq_word[:].bitcast(FP8X4), rhs_scale=xq_scale[:], start=True, stop=True,
+            )
+            tile = keep.tile([P, S], F32, name="y%d" % t)
+            nc.vector.tensor_copy(tile[:], bank[:])
+            y.append(tile)
+
+        h = [keep.tile([P, 2 * S], F32, name="h%d" % t) for t in range(PACK)]
+        st = [keep.tile([P, 2 * S], F32, name="st%d" % t) for t in range(PACK)]
+        pa = [keep.tile([P, W], F32, name="pa%d" % t) for t in range(PACK)]
+        pb = [keep.tile([P, W], F32, name="pb%d" % t) for t in range(PACK)]
+        rb = [keep.tile([P, W], F32, name="rb%d" % t) for t in range(PACK)]
+        top = [keep.tile([P, S], F32, name="top%d" % t) for t in range(PACK)]
+        zb = keep.tile([P, S, PACK], BF16, name="zb", align_bytes=64)
+
+        def fetch_pair(t):
+            nc.scalar.activation(pb[t][:], y[t][:].indirect(n2_t[:]), ACT.Copy)
+            nc.scalar.activation(pa[t][:], y[t][:].indirect(n1_t[:]), ACT.Copy)
+            nc.vector.tensor_tensor(rb[t][:], pa[t][:], pb[t][:], ALU.subtract)
+
+        def put_pb(t):
+            nc.scalar.activation(dt[t][:].indirect(n1_t[:]), pb[t][:], ACT.Copy)
+
+        def put_rb(t):
+            nc.scalar.activation(dt[t][:].indirect(n2_t[:]), rb[t][:], ACT.Copy)
+
+        def fetch_dt(t, a, b):
+            nc.scalar.activation(h[t][:, S + a:S + b], dt[t][:].indirect(n3_t[:, a // 16:b // 16]), ACT.Copy)
+
+        def take_larger(t, a, b):
+            nc.vector.scalar_tensor_tensor(
+                top[t][:, a:b], h[t][:, S + a:S + b], 0.5, dt[t][:, a:b], ALU.mult, ALU.max)
+
+        def weigh(t, a, b):
+            nc.vector.tensor_scalar(zb[:, a:b, t], top[t][:, a:b], gs_t[:, t:t + 1], None, ALU.mult)
+
+        dk_word_picked = keep.tile([P, H], U32, name="dk_word_picked", align_bytes=64)
+        dk_word = keep.tile([P, PACK, P], U32, name="dk_word", align_bytes=64)
+        dk_scale_picked = keep.tile([P, H], U8, name="dk_scale_picked", tag="w1_scale", align_bytes=64)
+        dk_scale_dealt = keep.tile([P, PACK, P], U8, name="dk_scale_dealt", align_bytes=64)
+        bias = keep.tile([P, PACK], F32, name="bias")
+
+        def pick_d_scales():
+            nc.vector.tensor_copy(dk_scale_picked[:], d_scale_tab[:].indirect(k1_t[:]))
+
+        def deal_d_scales():
+            nc.vector.tensor_copy(dk_scale_dealt[:], dk_scale_picked[:].rearrange("p (m t) -> p t m", t=PACK))
+            flat = dk_scale_dealt[:].rearrange("p t m -> p (t m)")
+            place_rows(dk_scale, flat, nc.sync)
+
+        def pick_d_words():
+            nc.vector.tensor_copy(dk_word_picked[:], d_word_tab[:].indirect(k1_t[:]))
+
+        def deal_d_words():
+            nc.vector.tensor_copy(dk_word[:], dk_word_picked[:].rearrange("p (m t) -> p t m", t=PACK))
+            nc.vector.scalar_tensor_tensor(bias[:], sl_t[:], -1.0, th_t[:], ALU.mult, ALU.mult)
+
+        dictionary_steps = [pick_d_scales, deal_d_scales, pick_d_words, deal_d_words]
+
+        last = PACK - 1
+        fetch_pair(0)
+        for t in range(PACK):
+            put_pb(t)
+            if t < last:
+                fetch_pair(t + 1)
+            if t > 0:
+                fetch_dt(t - 1, 0, S)
+                take_larger(t - 1, 0, S)
+                weigh(t - 1, 0, S)
+            put_rb(t)
+            dictionary_steps[t]()
+        halves = [(0, HALF), (HALF, S)]
+        for a, b in halves:
+            fetch_dt(last, a, b)
+        for a, b in halves:
+            take_larger(last, a, b)
+        for a, b in halves:
+            weigh(last, a, b)
+
+        z_word = keep.tile([P, S], U32, name="z_word", align_bytes=64)
+        z_scale = keep.tile([P, S], U8, name="z_scale", align_bytes=64)
+        for a, b in halves:
+            nc.vector.quantize_mx(
+                out=z_word[:, a:b].bitcast(FP8X4), scales=z_scale[:, a:b],
+                in_=zb[:, a:b, :].rearrange("p j t -> p (j t)"),
+            )
+        h_bank = {}
+        for t in range(PACK):
+            for c, (a, b) in enumerate(halves):
+                bank = psum.tile([P, HALF], F32, name="h_bank%d_%d" % (c, t), tag="bank%d" % (PACK * (1 - c) + t))
+                nc.tensor.matmul_mx(
+                    out=bank[:], lhsT=dk_word[:, t, :].bitcast(FP8X4), lhsT_scale=dk_scale[:, P * t:P * (t + 1)],
+                    rhs=z_word[:, a:b].bitcast(FP8X4), rhs_scale=z_scale[:, a:b], start=True, stop=True,
+                )
+                h_bank[c, t] = bank
+        for t in range(2):
+            nc.scalar.activation(h[t][:, 0:HALF], h_bank[0, t][:], ACT.Copy, scale=0.0625)
+
+        sg = [keep.tile([P, S], F32, name="sg%d" % t) for t in range(PACK)]
+        res = [keep.tile([P, S], F32, name="res%d" % t) for t in range(PACK)]
+        out_rows = out.rearrange("(p t) j -> p t j", t=PACK)
+
+        def fetch_h(t):
+            if t >= 2:
+                nc.vector.tensor_scalar(h[t][:, 0:HALF], h_bank[0, t][:], 0.0625, None, ALU.mult)
+            nc.vector.tensor_scalar(h[t][:, HALF:S], h_bank[1, t][:], 0.0625, None, ALU.mult)
+            nc.scalar.activation(st[t][:, S:2 * S], h[t][:].indirect(n4_t[:]), ACT.Copy)
+            nc.vector.tensor_tensor(st[t][:, 0:S], h[t][:, 0:S], st[t][:, S:2 * S], ALU.subtract)
+
+        def gate(t, a, b):
+            nc.scalar.activation(
+                sg[t][:, a:b], st[t][:].indirect(n5_t[:, a // 16:b // 16]), ACT.Sigmoid,
+                scale=sl_t[:, t:t + 1], bias=bias[:, t:t + 1])
+            nc.vector.tensor_tensor(res[t][:, a:b], h[t][:, a:b], sg[t][:, a:b], ALU.mult)
+            nc.sync.dma_start(out_rows[:, t, a:b], res[t][:, a:b])
+
+        fetch_h(0)
+        for t in range(PACK):
+            if t < last:
+                fetch_h(t + 1)
+                gate(t, 0, S)
+            else:
+                for a, b in halves:
+                    gate(t, a, b)

@@ -56,6 +56,10 @@ def tile_picked_hdenseswapdehq_none_p_kernel(
             nc.gpsimd.dma_start(tile[:], src.rearrange("(p t) o -> p (t o)", t=PACK))
             return tile
 
+        warm = keep.tile([P, 2], F32, name="warm")
+        nc.vector.memset(warm[:, 0:1], 0.0)
+        nc.scalar.activation(warm[:, 1:2], warm[:, 0:1], ACT.Sigmoid)
+
         w1_scale_raw = keep.tile([P, H], U8, name="w1_scale_raw", tag="w1_scale_raw", align_bytes=64)
         nc.vector.memset(w1_scale_raw[:].bitcast(I32), 0)
         x_scale_tab = keep.tile([P, T], U8, name="x_scale_tab", tag="x_scale_tab", align_bytes=64)

@@ -46,10 +46,8 @@ def tile_picked_hdenseswapdehq_none_p_kernel(
             queue.dma_start(tile[0:P:8, :].bitcast(I32), src[0].bitcast(I32))
 
         def place_rows(plane, picked, queue):
-            for s in range(1, 4):
-                queue.dma_start(plane[s:P:32, :].bitcast(I32), picked[8 * s:P:32, :].bitcast(I32))
             for q in range(4):
-                nc.vector.tensor_copy(plane[32 * q:32 * q + 1, :].bitcast(I32), picked[32 * q:32 * q + 1, :].bitcast(I32))
+                queue.dma_start(plane[32 * q:32 * q + 4, :].bitcast(I32), picked[32 * q:32 * q + 32:8, :].bitcast(I32))
 
         def load_column(src, name, tag):
             tile = keep.tile([P, PACK], F32, name=name, tag=tag, align_bytes=64)
@@ -60,20 +58,19 @@ def tile_picked_hdenseswapdehq_none_p_kernel(
         nc.vector.memset(warm[:, 0:1], 0.0)
         nc.scalar.activation(warm[:, 1:2], warm[:, 0:1], ACT.Sigmoid)
 
-        w1_scale_raw = keep.tile([P, H], U8, name="w1_scale_raw", tag="w1_scale_raw", align_bytes=64)
-        nc.vector.memset(w1_scale_raw[:].bitcast(I32), 0)
         x_scale_tab = keep.tile([P, T], U8, name="x_scale_tab", tag="x_scale_tab", align_bytes=64)
         nc.vector.memset(x_scale_tab[:].bitcast(I32), 0)
+        w1_scale_raw = keep.tile([P, H], U8, name="w1_scale_raw", tag="w1_scale_raw", align_bytes=64)
+        nc.vector.memset(w1_scale_raw[:].bitcast(I32), 0)
 
+        x_word_tab = load_words(x_words, nc.gpsimd, "x_word_tab")
+        w1_word_raw = keep.tile([P, 2 * H], U8, name="w1_word_raw", tag="w1_word_raw", align_bytes=64)
+        nc.gpsimd.dma_start(w1_word_raw[:].bitcast(I32), w1_words[0].bitcast(I32))
         offs_t = load_list(offs, "offs_t")
-        x_word_tab = load_words(x_words, nc.scalar, "x_word_tab")
-        load_scale_rows(x_scale_tab, x_scales, nc.sync)
+        load_scale_rows(x_scale_tab, x_scales, nc.scalar)
         w1_scale_rows = w1_scales[0].bitcast(I32)
         for q in range(4):
-            queue = nc.sync if q < 3 else nc.gpsimd
-            queue.dma_start(w1_scale_raw[32 * q:32 * q + 4, :].bitcast(I32), w1_scale_rows[4 * q:4 * q + 4, :])
-        w1_word_raw = keep.tile([P, 2 * H], U8, name="w1_word_raw", tag="w1_word_raw", align_bytes=64)
-        nc.sync.dma_start(w1_word_raw[:].bitcast(I32), w1_words[0].bitcast(I32))
+            nc.scalar.dma_start(w1_scale_raw[32 * q:32 * q + 4, :].bitcast(I32), w1_scale_rows[4 * q:4 * q + 4, :])
         n2_t = load_list(n2, "n2_t")
         n1_t = load_list(n1, "n1_t")
         n3_t = load_list(n3, "n3_t")
@@ -92,15 +89,15 @@ def tile_picked_hdenseswapdehq_none_p_kernel(
             dt.append(tile)
 
         d_scale_tab = keep.tile([P, T], U8, name="d_scale_tab", align_bytes=64)
-        nc.vector.memset(d_scale_tab[:].bitcast(I32), 0)
+        nc.gpsimd.memset(d_scale_tab[:].bitcast(I32), 0)
         load_scale_rows(d_scale_tab, d_scales, nc.gpsimd)
 
         xq_scale_picked = keep.tile([P, S], U8, name="xq_scale_picked", align_bytes=64)
         nc.vector.tensor_copy(xq_scale_picked[:], x_scale_tab[:].indirect(offs_t[:]))
-        place_rows(xq_scale, xq_scale_picked, nc.scalar)
+        place_rows(xq_scale, xq_scale_picked, nc.sync)
 
         w1_scale = keep.tile([P, PACK, P], U8, name="w1_scale", tag="w1_scale", align_bytes=64)
-        nc.vector.tensor_copy(w1_scale[:], w1_scale_raw[:].rearrange("p (m t) -> p t m", t=PACK))
+        nc.gpsimd.tensor_copy(w1_scale[:], w1_scale_raw[:].rearrange("p (m t) -> p t m", t=PACK))
         w1_word = []
         for t in range(PACK):
             tile = keep.tile([P, 2 * P], U8, name="w1_word%d" % t, align_bytes=64)
@@ -114,16 +111,20 @@ def tile_picked_hdenseswapdehq_none_p_kernel(
         sl_t = load_column(sl, "sl_t", "w1_scale_raw")
         th_t = load_column(th, "th_t", "w1_word_raw")
 
-        y = []
+        halves = [(0, HALF), (HALF, S)]
+        whole = [(0, S)]
+        y = [keep.tile([P, S], F32, name="y%d" % t) for t in range(PACK)]
         for t in range(PACK):
-            bank = psum.tile([P, S], F32, name="y_bank%d" % t, tag="bank%d" % t)
-            nc.tensor.matmul_mx(
-                out=bank[:], lhsT=w1_word[t][:].bitcast(FP4X4), lhsT_scale=w1_scale[:, t, :],
-                rhs=xq_word[:].bitcast(FP8X4), rhs_scale=xq_scale[:], start=True, stop=True,
-            )
-            tile = keep.tile([P, S], F32, name="y%d" % t)
-            nc.vector.tensor_copy(tile[:], bank[:])
-            y.append(tile)
+            for a, b in (halves if t == 0 else whole):
+                bank = psum.tile([P, b - a], F32, name="y_bank%d_%d" % (t, a), tag="bank%d" % (PACK if a else t))
+                nc.tensor.matmul_mx(
+                    out=bank[:], lhsT=w1_word[t][:].bitcast(FP4X4), lhsT_scale=w1_scale[:, t, :],
+                    rhs=xq_word[:, a:b].bitcast(FP8X4), rhs_scale=xq_scale[:, a:b], start=True, stop=True,
+                )
+                if a:
+                    nc.scalar.copy(y[t][:, a:b], bank[:])
+                else:
+                    nc.vector.tensor_copy(y[t][:, a:b], bank[:])
 
         h = [keep.tile([P, 2 * S], F32, name="h%d" % t) for t in range(PACK)]
         st = [keep.tile([P, 2 * S], F32, name="st%d" % t) for t in range(PACK)]
@@ -189,7 +190,6 @@ def tile_picked_hdenseswapdehq_none_p_kernel(
                 weigh(t - 1, 0, S)
             put_rb(t)
             dictionary_steps[t]()
-        halves = [(0, HALF), (HALF, S)]
         for a, b in halves:
             fetch_dt(last, a, b)
         for a, b in halves:
@@ -206,24 +206,24 @@ def tile_picked_hdenseswapdehq_none_p_kernel(
             )
         h_bank = {}
         for t in range(PACK):
-            for c, (a, b) in enumerate(halves):
-                bank = psum.tile([P, HALF], F32, name="h_bank%d_%d" % (c, t), tag="bank%d" % (PACK * (1 - c) + t))
+            for a, b in (halves if t == 0 else whole):
+                bank = psum.tile([P, b - a], F32, name="h_bank%d_%d" % (t, a), tag="bank%d" % (PACK if a else t))
                 nc.tensor.matmul_mx(
                     out=bank[:], lhsT=dk_word[:, t, :].bitcast(FP8X4), lhsT_scale=dk_scale[:, P * t:P * (t + 1)],
                     rhs=z_word[:, a:b].bitcast(FP8X4), rhs_scale=z_scale[:, a:b], start=True, stop=True,
                 )
-                h_bank[c, t] = bank
-        for t in range(2):
-            nc.scalar.activation(h[t][:, 0:HALF], h_bank[0, t][:], ACT.Copy, scale=0.0625)
+                h_bank[t, a] = bank
 
         sg = [keep.tile([P, S], F32, name="sg%d" % t) for t in range(PACK)]
         res = [keep.tile([P, S], F32, name="res%d" % t) for t in range(PACK)]
         out_rows = out.rearrange("(p t) j -> p t j", t=PACK)
 
         def fetch_h(t):
-            if t >= 2:
-                nc.vector.tensor_scalar(h[t][:, 0:HALF], h_bank[0, t][:], 0.0625, None, ALU.mult)
-            nc.vector.tensor_scalar(h[t][:, HALF:S], h_bank[1, t][:], 0.0625, None, ALU.mult)
+            if t == 0:
+                nc.scalar.activation(h[t][:, 0:HALF], h_bank[t, 0][:], ACT.Copy, scale=0.0625)
+                nc.vector.tensor_scalar(h[t][:, HALF:S], h_bank[t, HALF][:], 0.0625, None, ALU.mult)
+            else:
+                nc.vector.tensor_scalar(h[t][:, 0:S], h_bank[t, 0][:], 0.0625, None, ALU.mult)
             nc.scalar.activation(st[t][:, S:2 * S], h[t][:].indirect(n4_t[:]), ACT.Copy)
             nc.vector.tensor_tensor(st[t][:, 0:S], h[t][:, 0:S], st[t][:, S:2 * S], ALU.subtract)
 
@@ -234,11 +234,11 @@ def tile_picked_hdenseswapdehq_none_p_kernel(
             nc.vector.tensor_tensor(res[t][:, a:b], h[t][:, a:b], sg[t][:, a:b], ALU.mult)
             nc.sync.dma_start(out_rows[:, t, a:b], res[t][:, a:b])
 
-        fetch_h(0)
+        ahead = 2
+        for t in range(ahead):
+            fetch_h(t)
         for t in range(PACK):
-            if t < last:
-                fetch_h(t + 1)
-                gate(t, 0, S)
-            else:
-                for a, b in halves:
-                    gate(t, a, b)
+            if t + ahead < PACK:
+                fetch_h(t + ahead)
+            for a, b in (halves if t == last else whole):
+                gate(t, a, b)

@@ -82,22 +82,19 @@ def tile_picked_hdenseswapdehq_none_p_kernel(
         nc.vector.memset(xq_scale[:].bitcast(I32), 0)
         dk_scale = keep.tile([P, H], U8, name="dk_scale", align_bytes=64)
         nc.vector.memset(dk_scale[:].bitcast(I32), 0)
-        dt = []
-        for t in range(PACK):
-            tile = keep.tile([P, S + SPARE], F32, name="dt%d" % t)
-            nc.vector.memset(tile[:, S:], 0.0)
-            dt.append(tile)
+        dt = [keep.tile([P, S + SPARE], F32, name="dt%d" % t) for t in range(PACK)]
 
         d_scale_tab = keep.tile([P, T], U8, name="d_scale_tab", align_bytes=64)
         nc.gpsimd.memset(d_scale_tab[:].bitcast(I32), 0)
         load_scale_rows(d_scale_tab, d_scales, nc.gpsimd)
 
-        xq_scale_picked = keep.tile([P, S], U8, name="xq_scale_picked", align_bytes=64)
+        xq_scale_picked = keep.tile([P, S], U8, name="xq_scale_picked", tag="xq_scale_picked", align_bytes=64)
         nc.vector.tensor_copy(xq_scale_picked[:], x_scale_tab[:].indirect(offs_t[:]))
         place_rows(xq_scale, xq_scale_picked, nc.sync)
 
-        w1_scale = keep.tile([P, PACK, P], U8, name="w1_scale", tag="w1_scale", align_bytes=64)
-        nc.gpsimd.tensor_copy(w1_scale[:], w1_scale_raw[:].rearrange("p (m t) -> p t m", t=PACK))
+        w1_scale_by_tile = w1_scale_raw[:].rearrange("p (m t) -> p t m", t=PACK)
+        w1_scale_first = keep.tile([P, P], U8, name="w1_scale_first", align_bytes=64)
+        nc.vector.tensor_copy(w1_scale_first[:], w1_scale_by_tile[:, 0, :])
         w1_word = []
         for t in range(PACK):
             tile = keep.tile([P, 2 * P], U8, name="w1_word%d" % t, align_bytes=64)
@@ -106,6 +103,9 @@ def tile_picked_hdenseswapdehq_none_p_kernel(
 
         xq_word = keep.tile([P, S], U32, name="xq_word", align_bytes=64)
         nc.vector.tensor_copy(xq_word[:], x_word_tab[:].indirect(offs_t[:]))
+        w1_scale_rest = keep.tile([P, PACK - 1, P], U8, name="w1_scale_rest", tag="xq_scale_picked", align_bytes=64)
+        nc.vector.tensor_copy(w1_scale_rest[:], w1_scale_by_tile[:, 1:PACK, :])
+        w1_scale = [w1_scale_first[:]] + [w1_scale_rest[:, t, :] for t in range(PACK - 1)]
         d_word_tab = load_words(d_words, nc.sync, "d_word_tab")
         gs_t = load_column(gs, "gs_t", "x_scale_tab")
         sl_t = load_column(sl, "sl_t", "w1_scale_raw")
@@ -118,7 +118,7 @@ def tile_picked_hdenseswapdehq_none_p_kernel(
             for a, b in (halves if t == 0 else whole):
                 bank = psum.tile([P, b - a], F32, name="y_bank%d_%d" % (t, a), tag="bank%d" % (PACK if a else t))
                 nc.tensor.matmul_mx(
-                    out=bank[:], lhsT=w1_word[t][:].bitcast(FP4X4), lhsT_scale=w1_scale[:, t, :],
+                    out=bank[:], lhsT=w1_word[t][:].bitcast(FP4X4), lhsT_scale=w1_scale[t],
                     rhs=xq_word[:, a:b].bitcast(FP8X4), rhs_scale=xq_scale[:, a:b], start=True, stop=True,
                 )
                 if a:
@@ -157,7 +157,7 @@ def tile_picked_hdenseswapdehq_none_p_kernel(
 
         dk_word_picked = keep.tile([P, H], U32, name="dk_word_picked", align_bytes=64)
         dk_word = keep.tile([P, PACK, P], U32, name="dk_word", align_bytes=64)
-        dk_scale_picked = keep.tile([P, H], U8, name="dk_scale_picked", tag="w1_scale", align_bytes=64)
+        dk_scale_picked = keep.tile([P, H], U8, name="dk_scale_picked", tag="xq_scale_picked", align_bytes=64)
         dk_scale_dealt = keep.tile([P, PACK, P], U8, name="dk_scale_dealt", align_bytes=64)
         bias = keep.tile([P, PACK], F32, name="bias")
 

@@ -51,15 +51,16 @@ def tile_picked_hdenseswapdehq_none_p_kernel(
 
         def load_column(src, name, tag):
             tile = keep.tile([P, PACK], F32, name=name, tag=tag, align_bytes=64)
-            nc.gpsimd.dma_start(tile[:], src.rearrange("(p t) o -> p (t o)", t=PACK))
+            nc.sync.dma_start(tile[:], src.rearrange("(p t) o -> p (t o)", t=PACK))
             return tile
+
+        x_scale_tab = keep.tile([P, T], U8, name="x_scale_tab", tag="x_scale_tab", align_bytes=64)
+        nc.vector.memset(x_scale_tab[:].bitcast(I32), 0)
 
         warm = keep.tile([P, 2], F32, name="warm")
         nc.vector.memset(warm[:, 0:1], 0.0)
         nc.scalar.activation(warm[:, 1:2], warm[:, 0:1], ACT.Sigmoid)
 
-        x_scale_tab = keep.tile([P, T], U8, name="x_scale_tab", tag="x_scale_tab", align_bytes=64)
-        nc.vector.memset(x_scale_tab[:].bitcast(I32), 0)
         w1_scale_raw = keep.tile([P, H], U8, name="w1_scale_raw", tag="w1_scale_raw", align_bytes=64)
         nc.vector.memset(w1_scale_raw[:].bitcast(I32), 0)
 
@@ -84,16 +85,16 @@ def tile_picked_hdenseswapdehq_none_p_kernel(
         nc.vector.memset(dk_scale[:].bitcast(I32), 0)
         dt = [keep.tile([P, S + SPARE], F32, name="dt%d" % t) for t in range(PACK)]
 
-        d_scale_tab = keep.tile([P, T], U8, name="d_scale_tab", align_bytes=64)
-        nc.gpsimd.memset(d_scale_tab[:].bitcast(I32), 0)
-        load_scale_rows(d_scale_tab, d_scales, nc.gpsimd)
-
         xq_scale_picked = keep.tile([P, S], U8, name="xq_scale_picked", tag="xq_scale_picked", align_bytes=64)
         nc.vector.tensor_copy(xq_scale_picked[:], x_scale_tab[:].indirect(offs_t[:]))
         place_rows(xq_scale, xq_scale_picked, nc.sync)
 
+        d_scale_tab = keep.tile([P, T], U8, name="d_scale_tab", tag="x_scale_tab", align_bytes=64)
+        nc.vector.memset(d_scale_tab[:].bitcast(I32), 0)
+        load_scale_rows(d_scale_tab, d_scales, nc.sync)
+
         w1_scale_by_tile = w1_scale_raw[:].rearrange("p (m t) -> p t m", t=PACK)
-        w1_scale_first = keep.tile([P, P], U8, name="w1_scale_first", align_bytes=64)
+        w1_scale_first = keep.tile([P, P], U8, name="w1_scale_first", tag="w1_scale_first", align_bytes=64)
         nc.vector.tensor_copy(w1_scale_first[:], w1_scale_by_tile[:, 0, :])
         w1_word = []
         for t in range(PACK):
@@ -107,9 +108,8 @@ def tile_picked_hdenseswapdehq_none_p_kernel(
         nc.vector.tensor_copy(w1_scale_rest[:], w1_scale_by_tile[:, 1:PACK, :])
         w1_scale = [w1_scale_first[:]] + [w1_scale_rest[:, t, :] for t in range(PACK - 1)]
         d_word_tab = load_words(d_words, nc.sync, "d_word_tab")
-        gs_t = load_column(gs, "gs_t", "x_scale_tab")
+        gs_t = load_column(gs, "gs_t", "w1_word_raw")
         sl_t = load_column(sl, "sl_t", "w1_scale_raw")
-        th_t = load_column(th, "th_t", "w1_word_raw")
 
         halves = [(0, HALF), (HALF, S)]
         whole = [(0, S)]
@@ -126,6 +126,7 @@ def tile_picked_hdenseswapdehq_none_p_kernel(
                 else:
                     nc.vector.tensor_copy(y[t][:, a:b], bank[:])
 
+        th_t = load_column(th, "th_t", "w1_scale_first")
         h = [keep.tile([P, 2 * S], F32, name="h%d" % t) for t in range(PACK)]
         st = [keep.tile([P, 2 * S], F32, name="st%d" % t) for t in range(PACK)]
         pa = [keep.tile([P, W], F32, name="pa%d" % t) for t in range(PACK)]

from contextlib import ExitStack

import concourse.mybir as mybir

K, T, S, H, W = 512, 2048, 256, 512, 128
FLOPS = 2 * K * H * S * 2

F32 = mybir.dt.float32
BF16 = mybir.dt.bfloat16
I32 = mybir.dt.int32
U32 = mybir.dt.uint32
U16 = mybir.dt.uint16
U8 = mybir.dt.uint8
FP8X4 = mybir.dt.float8_e4m3fn_x4
FP4X4 = mybir.dt.float4_e2m1fn_x4
ALU = mybir.AluOpType
ACT = mybir.ActivationFunctionType

P = 128
PACK = 4
HALF = S // 2
SPARE = 16


def tile_picked_hdenseswapdehq_none_p_kernel(
    tc, x_words, x_scales, w1_words, w1_scales, gs, d_words, d_scales, sl, th,
    offs, n1, n2, n3, k1, n4, n5, out,
):
    nc = tc.nc
    with ExitStack() as ctx:
        lists = ctx.enter_context(tc.tile_pool(name="lists", bufs=1))
        keep = ctx.enter_context(tc.tile_pool(name="keep", bufs=1))
        psum = ctx.enter_context(tc.psum_pool(name="psum", bufs=1))

        def load_list(src, name):
            tile = lists.tile(list(src.shape), U16, name=name)
            nc.sync.dma_start(tile[:], src)
            return tile

        def load_words(src, queue, name):
            tile = keep.tile([P, T], U32, name=name, tag="table_words", align_bytes=64)
            queue.dma_start(tile[:].bitcast(I32), src[0].rearrange("p c r -> p (c r)").bitcast(I32))
            return tile

        def load_scale_rows(tile, src, queue):
            queue.dma_start(tile[0:P:8, :].bitcast(I32), src[0].bitcast(I32))

        def place_rows(plane, picked, queue):
            for q in range(4):
                queue.dma_start(plane[32 * q:32 * q + 4, :].bitcast(I32), picked[32 * q:32 * q + 32:8, :].bitcast(I32))

        def load_column(src, name, tag):
            tile = keep.tile([P, PACK], F32, name=name, tag=tag, align_bytes=64)
            nc.sync.dma_start(tile[:], src.rearrange("(p t) o -> p (t o)", t=PACK))
            return tile

        x_scale_tab = keep.tile([P, T], U8, name="x_scale_tab", tag="x_scale_tab", align_bytes=64)
        nc.vector.memset(x_scale_tab[:].bitcast(I32), 0)

        warm = keep.tile([P, 2], F32, name="warm")
        nc.vector.memset(warm[:, 0:1], 0.0)
        nc.scalar.activation(warm[:, 1:2], warm[:, 0:1], ACT.Sigmoid)

        w1_scale_raw = keep.tile([P, H], U8, name="w1_scale_raw", tag="w1_scale_raw", align_bytes=64)
        nc.vector.memset(w1_scale_raw[:].bitcast(I32), 0)

        x_word_tab = load_words(x_words, nc.gpsimd, "x_word_tab")
        w1_word_raw = keep.tile([P, 2 * H], U8, name="w1_word_raw", tag="w1_word_raw", align_bytes=64)
        nc.gpsimd.dma_start(w1_word_raw[:].bitcast(I32), w1_words[0].bitcast(I32))
        offs_t = load_list(offs, "offs_t")
        load_scale_rows(x_scale_tab, x_scales, nc.scalar)
        w1_scale_rows = w1_scales[0].bitcast(I32)
        for q in range(4):
            nc.scalar.dma_start(w1_scale_raw[32 * q:32 * q + 4, :].bitcast(I32), w1_scale_rows[4 * q:4 * q + 4, :])
        n2_t = load_list(n2, "n2_t")
        n1_t = load_list(n1, "n1_t")
        n3_t = load_list(n3, "n3_t")
        k1_t = load_list(k1, "k1_t")
        n4_t = load_list(n4, "n4_t")
        n5_t = load_list(n5, "n5_t")

        xq_scale = keep.tile([P, S], U8, name="xq_scale", align_bytes=64)
        nc.vector.memset(xq_scale[:].bitcast(I32), 0)
        dk_scale = keep.tile([P, H], U8, name="dk_scale", align_bytes=64)
        nc.vector.memset(dk_scale[:].bitcast(I32), 0)
        dt = [keep.tile([P, S + SPARE], F32, name="dt%d" % t) for t in range(PACK)]

        xq_scale_picked = keep.tile([P, S], U8, name="xq_scale_picked", tag="xq_scale_picked", align_bytes=64)
        nc.vector.tensor_copy(xq_scale_picked[:], x_scale_tab[:].indirect(offs_t[:]))
        place_rows(xq_scale, xq_scale_picked, nc.sync)

        d_scale_tab = keep.tile([P, T], U8, name="d_scale_tab", tag="x_scale_tab", align_bytes=64)
        nc.vector.memset(d_scale_tab[:].bitcast(I32), 0)
        load_scale_rows(d_scale_tab, d_scales, nc.sync)

        w1_scale_by_tile = w1_scale_raw[:].rearrange("p (m t) -> p t m", t=PACK)
        w1_scale_first = keep.tile([P, P], U8, name="w1_scale_first", tag="w1_scale_first", align_bytes=64)
        nc.vector.tensor_copy(w1_scale_first[:], w1_scale_by_tile[:, 0, :])
        w1_word = []
        for t in range(PACK):
            tile = keep.tile([P, 2 * P], U8, name="w1_word%d" % t, align_bytes=64)
            nc.scalar.copy(tile[:].bitcast(U16), w1_word_raw[:].bitcast(U16)[:, t:H:PACK])
            w1_word.append(tile)

        xq_word = keep.tile([P, S], U32, name="xq_word", align_bytes=64)
        nc.vector.tensor_copy(xq_word[:], x_word_tab[:].indirect(offs_t[:]))
        w1_scale_rest = keep.tile([P, PACK - 1, P], U8, name="w1_scale_rest", tag="xq_scale_picked", align_bytes=64)
        nc.vector.tensor_copy(w1_scale_rest[:], w1_scale_by_tile[:, 1:PACK, :])
        w1_scale = [w1_scale_first[:]] + [w1_scale_rest[:, t, :] for t in range(PACK - 1)]
        d_word_tab = load_words(d_words, nc.sync, "d_word_tab")
        gs_t = load_column(gs, "gs_t", "w1_word_raw")
        sl_t = load_column(sl, "sl_t", "w1_scale_raw")

        halves = [(0, HALF), (HALF, S)]
        whole = [(0, S)]
        y = [keep.tile([P, S], F32, name="y%d" % t) for t in range(PACK)]
        for t in range(PACK):
            for a, b in (halves if t == 0 else whole):
                bank = psum.tile([P, b - a], F32, name="y_bank%d_%d" % (t, a), tag="bank%d" % (PACK if a else t))
                nc.tensor.matmul_mx(
                    out=bank[:], lhsT=w1_word[t][:].bitcast(FP4X4), lhsT_scale=w1_scale[t],
                    rhs=xq_word[:, a:b].bitcast(FP8X4), rhs_scale=xq_scale[:, a:b], start=True, stop=True,
                )
                if a:
                    nc.scalar.copy(y[t][:, a:b], bank[:])
                else:
                    nc.vector.tensor_copy(y[t][:, a:b], bank[:])

        th_t = load_column(th, "th_t", "w1_scale_first")
        h = [keep.tile([P, 2 * S], F32, name="h%d" % t) for t in range(PACK)]
        st = [keep.tile([P, 2 * S], F32, name="st%d" % t) for t in range(PACK)]
        pa = [keep.tile([P, W], F32, name="pa%d" % t) for t in range(PACK)]
        pb = [keep.tile([P, W], F32, name="pb%d" % t) for t in range(PACK)]
        rb = [keep.tile([P, W], F32, name="rb%d" % t) for t in range(PACK)]
        top = [keep.tile([P, S], F32, name="top%d" % t) for t in range(PACK)]
        zb = keep.tile([P, S, PACK], BF16, name="zb", align_bytes=64)

        def fetch_pair(t):
            nc.scalar.activation(pb[t][:], y[t][:].indirect(n2_t[:]), ACT.Copy)
            nc.scalar.activation(pa[t][:], y[t][:].indirect(n1_t[:]), ACT.Copy)
            nc.vector.tensor_tensor(rb[t][:], pa[t][:], pb[t][:], ALU.subtract)

        def put_pb(t):
            nc.scalar.activation(dt[t][:].indirect(n1_t[:]), pb[t][:], ACT.Copy)

        def put_rb(t):
            nc.scalar.activation(dt[t][:].indirect(n2_t[:]), rb[t][:], ACT.Copy)

        def fetch_dt(t, a, b):
            nc.scalar.activation(h[t][:, S + a:S + b], dt[t][:].indirect(n3_t[:, a // 16:b // 16]), ACT.Copy)

        def take_larger(t, a, b):
            nc.vector.scalar_tensor_tensor(
                top[t][:, a:b], h[t][:, S + a:S + b], 0.5, dt[t][:, a:b], ALU.mult, ALU.max)

        def weigh(t, a, b):
            nc.vector.tensor_scalar(zb[:, a:b, t], top[t][:, a:b], gs_t[:, t:t + 1], None, ALU.mult)

        dk_word_picked = keep.tile([P, H], U32, name="dk_word_picked", align_bytes=64)
        dk_word = keep.tile([P, PACK, P], U32, name="dk_word", align_bytes=64)
        dk_scale_picked = keep.tile([P, H], U8, name="dk_scale_picked", tag="xq_scale_picked", align_bytes=64)
        dk_scale_dealt = keep.tile([P, PACK, P], U8, name="dk_scale_dealt", align_bytes=64)
        bias = keep.tile([P, PACK], F32, name="bias")

        def pick_d_scales():
            nc.vector.tensor_copy(dk_scale_picked[:], d_scale_tab[:].indirect(k1_t[:]))

        def deal_d_scales():
            nc.vector.tensor_copy(dk_scale_dealt[:], dk_scale_picked[:].rearrange("p (m t) -> p t m", t=PACK))
            flat = dk_scale_dealt[:].rearrange("p t m -> p (t m)")
            place_rows(dk_scale, flat, nc.sync)

        def pick_d_words():
            nc.vector.tensor_copy(dk_word_picked[:], d_word_tab[:].indirect(k1_t[:]))

        def deal_d_words():
            nc.vector.tensor_copy(dk_word[:], dk_word_picked[:].rearrange("p (m t) -> p t m", t=PACK))
            nc.vector.scalar_tensor_tensor(bias[:], sl_t[:], -1.0, th_t[:], ALU.mult, ALU.mult)

        dictionary_steps = [pick_d_scales, deal_d_scales, pick_d_words, deal_d_words]

        last = PACK - 1
        fetch_pair(0)
        for t in range(PACK):
            put_pb(t)
            if t < last:
                fetch_pair(t + 1)
            if t > 0:
                fetch_dt(t - 1, 0, S)
                take_larger(t - 1, 0, S)
                weigh(t - 1, 0, S)
            put_rb(t)
            dictionary_steps[t]()
        for a, b in halves:
            fetch_dt(last, a, b)
        for a, b in halves:
            take_larger(last, a, b)
        for a, b in halves:
            weigh(last, a, b)

        z_word = keep.tile([P, S], U32, name="z_word", align_bytes=64)
        z_scale = keep.tile([P, S], U8, name="z_scale", align_bytes=64)
        for a, b in halves:
            nc.vector.quantize_mx(
                out=z_word[:, a:b].bitcast(FP8X4), scales=z_scale[:, a:b],
                in_=zb[:, a:b, :].rearrange("p j t -> p (j t)"),
            )
        h_bank = {}
        for t in range(PACK):
            for a, b in (halves if t == 0 else whole):
                bank = psum.tile([P, b - a], F32, name="h_bank%d_%d" % (t, a), tag="bank%d" % (PACK if a else t))
                nc.tensor.matmul_mx(
                    out=bank[:], lhsT=dk_word[:, t, :].bitcast(FP8X4), lhsT_scale=dk_scale[:, P * t:P * (t + 1)],
                    rhs=z_word[:, a:b].bitcast(FP8X4), rhs_scale=z_scale[:, a:b], start=True, stop=True,
                )
                h_bank[t, a] = bank

        sg = [keep.tile([P, S], F32, name="sg%d" % t) for t in range(PACK)]
        res = [keep.tile([P, S], F32, name="res%d" % t) for t in range(PACK)]
        out_rows = out.rearrange("(p t) j -> p t j", t=PACK)

        def fetch_h(t):
            if t == 0:
                nc.scalar.activation(h[t][:, 0:HALF], h_bank[t, 0][:], ACT.Copy, scale=0.0625)
                nc.vector.tensor_scalar(h[t][:, HALF:S], h_bank[t, HALF][:], 0.0625, None, ALU.mult)
            else:
                nc.vector.tensor_scalar(h[t][:, 0:S], h_bank[t, 0][:], 0.0625, None, ALU.mult)
            nc.scalar.activation(st[t][:, S:2 * S], h[t][:].indirect(n4_t[:]), ACT.Copy)
            nc.vector.tensor_tensor(st[t][:, 0:S], h[t][:, 0:S], st[t][:, S:2 * S], ALU.subtract)

        def gate(t, a, b):
            nc.scalar.activation(
                sg[t][:, a:b], st[t][:].indirect(n5_t[:, a // 16:b // 16]), ACT.Sigmoid,
                scale=sl_t[:, t:t + 1], bias=bias[:, t:t + 1])
            nc.vector.tensor_tensor(res[t][:, a:b], h[t][:, a:b], sg[t][:, a:b], ALU.mult)
            nc.sync.dma_start(out_rows[:, t, a:b], res[t][:, a:b])

        ahead = 2
        for t in range(ahead):
            fetch_h(t)
        for t in range(PACK):
            if t + ahead < PACK:
                fetch_h(t + ahead)
            for a, b in (halves if t == last else whole):
                gate(t, a, b)
